import numpy as np
import ml_dtypes


def mxq(x, axis, fmt="e4m3"):
    dtype, down = {"e4m3": (ml_dtypes.float8_e4m3fn, 7), "e5m2": (ml_dtypes.float8_e5m2, 14)}[fmt]
    v = np.moveaxis(np.asarray(x, np.float32).astype(ml_dtypes.bfloat16).astype(np.float64), axis, -1)
    blocks = v.reshape(v.shape[:-1] + (-1, 32))
    amax = np.abs(blocks).max(-1, keepdims=True)
    byte = np.maximum(np.where(amax > 0, np.frexp(amax)[1] - 1 + 127, 0) - down, 1)
    scale = np.exp2(byte - 127.0)
    codes = (blocks / scale).astype(np.float32).astype(dtype).astype(np.float64)
    return np.moveaxis((codes * scale).reshape(v.shape), -1, axis)


WIDE = False


def mx_kscale(k):
    if not WIDE:
        return np.ones(k)
    levels = np.array([10, -10, 5, -5, 0])
    if k % 512:
        return np.exp2(np.random.permutation(np.resize(levels, k // 32))).repeat(32)
    a = np.empty((k // 512, 16))
    for p in range(k // 512):
        a[p, :8] = np.random.permutation(np.resize(levels, 8))
        for g in range(8):
            far = levels[np.abs(levels - a[p, g]) >= 10]
            a[p, g + 8] = far[np.random.randint(len(far))]
    return np.exp2(a.ravel()).repeat(32)


def f64(x):
    return np.asarray(x).astype(np.float64)


def striped(idx):
    return np.tile(idx.reshape(-1, 16).T, (8, 1)).astype(np.uint16)


def unstriped(offs):
    return offs[:16].T.reshape(-1).astype(np.int64)


def pack_weight(w):
    k, n = w.shape
    w = f64(np.asarray(w, np.float32).astype(ml_dtypes.bfloat16)).reshape(k // 32, 32, n)
    amax = np.abs(w).max(1)
    byte = np.clip(np.where(amax > 0, np.frexp(amax)[1] - 1 + 127 - 7, 1), 1, 254)
    scaled = (w * np.exp2(127.0 - byte)[:, None, :]).reshape(k, n).astype(np.float32)
    words = np.ascontiguousarray(scaled.reshape(k // 512, 128, 4, n).transpose(0, 1, 3, 2)).astype(ml_dtypes.float8_e4m3fn).view(np.uint8)
    return words, np.ascontiguousarray(byte.astype(np.uint8).reshape(k // 512, 16, n))


def unpack_weight(words, scales):
    g, p, n, _ = words.shape
    vals = np.ascontiguousarray(words).view(ml_dtypes.float8_e4m3fn).astype(np.float64) * np.repeat(np.exp2(scales.astype(np.float64) - 127.0), 8, axis=1)[..., None]
    return vals.transpose(0, 1, 3, 2).reshape(g * 512, n)


K, T, S, V, R = 512, 1024, 512, 512, 512
P = 2 ** 7


def setup_inputs():
    n = np.random.standard_normal
    s = mx_kscale(K)[:, None]
    packed_xT = pack_weight(n((K, T)) * s)
    return {
        "x_words": packed_xT[0],
        "x_scales": packed_xT[1],
        "hT": (n((K, V)) / np.sqrt(K) / s).astype(np.float32),
        "alpha": (n((V, R))).astype(np.float32),
        "m1": (np.tile((np.random.uniform(size=R) < 0.8) * 1.0, (P, 1))).astype(np.float32),
        "m2": (np.tile((np.random.uniform(size=R) < 0.4) * 1.0, (P, 1))).astype(np.float32),
        "offs": striped(np.random.permutation(T)[:S]),
        "lab": striped(np.random.randint(0, S, R)),
    }


def reference(x_words, x_scales, hT, alpha, m1, m2, offs, lab):
    hTq = mxq(f64(hT), 0, "e4m3")
    xq = unpack_weight(x_words, x_scales)[:, unstriped(offs)]
    y = hTq.T @ xq
    ee = np.exp(y)
    s0 = np.log(ee.sum(axis=1, keepdims=True))
    lp = y - s0
    gg = lp[:, unstriped(lab)]
    ea = np.exp(f64(alpha))
    return gg + np.log(ea + (np.pad(ea, ((0, 0), (1, 0)))[:, :S]) * f64(m1)[:1] + (np.pad(ea, ((0, 0), (2, 0)))[:, :S]) * f64(m2)[:1])

@@ -1,0 +1,147 @@
+from contextlib import ExitStack
+
+import concourse.mybir as mybir
+from concourse.masks import make_identity
+
+F32 = mybir.dt.float32
+BF16 = mybir.dt.bfloat16
+I32 = mybir.dt.int32
+U32 = mybir.dt.uint32
+U16 = mybir.dt.uint16
+U8 = mybir.dt.uint8
+FP8X4 = mybir.dt.float8_e4m3fn_x4
+ALU = mybir.AluOpType
+ACT = mybir.ActivationFunctionType
+AX = mybir.AxisListType
+
+P = 128
+PACK = 4
+K, T, S, V, R = 512, 1024, 512, 512, 512
+TILES = V // P
+BLOCKS = R // P
+HALVES = 2
+HALF = V // HALVES
+PAD = 16
+LN_SCALE = 2.0**54
+
+POOL_MASKS = [(0, 1),(0, 2),(1, 1),(1, 2),(2, 1),(2, 2),(3, 1),(3, 2)]
+FUSED = []
+PIECE = R // 2
+
+FLOPS = 2 * K * V * S
+
+
+def tile_picked_yctc_log_p_kernel(tc, x_words, x_scales, hT, alpha, m1, m2, offs, lab, out):
+    nc = tc.nc
+    with ExitStack() as ctx:
+        keep = ctx.enter_context(tc.tile_pool(name="keep", bufs=1))
+        psum = ctx.enter_context(tc.psum_pool(name="psum", bufs=1))
+
+        offs_sb = keep.tile([P, S // 16], U16, name="offs_sb")
+        lab_sb = keep.tile([P, R // 16], U16, name="lab_sb")
+        words_all = keep.tile([P, T], I32, name="words_all", align_bytes=64)
+        scales_all = keep.tile([P, T], U8, name="scales_all", align_bytes=64)
+        words = keep.tile([P, S], U32, name="words", align_bytes=64)
+        scales = keep.tile([P, S], U8, name="scales", align_bytes=64)
+        ident = keep.tile([P, P], F32, name="ident")
+        warm = keep.tile([P, 2], F32, name="warm")
+
+        nc.gpsimd.memset(scales_all[:].bitcast(I32), 0)
+        nc.vector.memset(warm[:, 0:1], 0.0)
+        nc.scalar.activation(warm[:, 1:2], warm[:, 0:1], ACT.Exp)
+
+        h_view = hT.rearrange("(p j) t -> p j t", j=PACK)
+        h_raw = [keep.tile([P, PACK, HALF], F32, name="h_raw%d" % u) for u in range(HALVES)]
+        a_sb = [keep.tile([P, R], F32, name="a_sb%d" % i) for i in range(TILES)]
+        m1_sb = keep.tile([P, R], F32, name="m1_sb")
+        m2_sb = keep.tile([P, R], F32, name="m2_sb")
+        nc.sync.dma_start(offs_sb[:], offs)
+        nc.sync.dma_start(a_sb[0][:], alpha[0 * P : 1 * P, :])
+        for q in range(4):
+            nc.scalar.dma_start(scales_all[32 * q : 32 * q + 4, :].bitcast(I32), x_scales[0, 4 * q : 4 * q + 4, :].bitcast(I32))
+        nc.sync.dma_start(m1_sb[:], m1)
+        nc.sync.dma_start(words_all[:], x_words[0].rearrange("p n t -> p (n t)").bitcast(I32))
+        nc.sync.dma_start(m2_sb[:], m2)
+        nc.sync.dma_start(h_raw[0][:], h_view[:, :, 0 * HALF : 1 * HALF])
+        nc.sync.dma_start(a_sb[1][:], alpha[1 * P : 2 * P, :])
+        nc.sync.dma_start(h_raw[1][:], h_view[:, :, 1 * HALF : 2 * HALF])
+        nc.sync.dma_start(a_sb[2][:], alpha[2 * P : 3 * P, :])
+        nc.sync.dma_start(a_sb[3][:], alpha[3 * P : 4 * P, :])
+        nc.sync.dma_start(lab_sb[:], lab)
+
+        make_identity(nc, ident[:])
+        ea = keep.tile([P, TILES, PAD + R], F32, name="ea")
+        nc.gpsimd.memset(ea[:, :, PAD - 2 : PAD], 0.0)
+        y_sb = [keep.tile([P, S], F32, name="y_sb%d" % i) for i in range(TILES)]
+
+        nc.vector.tensor_copy(scales[:], scales_all[:].indirect(offs_sb[:]))
+        nc.vector.tensor_copy(words[:], words_all[:].bitcast(U32).indirect(offs_sb[:]))
+
+        stats = keep.tile([P, TILES, 4], F32, name="stats")
+        neg_ymax = keep.tile([P, TILES], F32, name="neg_ymax")
+        sums = keep.tile([P, TILES], F32, name="sums")
+        shift = keep.tile([P, TILES], F32, name="shift")
+
+        h_codes = keep.tile([P, V], U32, name="h_codes", align_bytes=64)
+        h_scales = keep.tile([P, V], U8, name="h_scales", align_bytes=64)
+        for u in range(HALVES):
+            grouped = keep.tile([P, HALF, PACK], BF16, name="grouped%d" % u, align_bytes=64)
+            nc.scalar.copy(grouped[:].rearrange("p (c i) j -> p c j i", i=4), h_raw[u][:].rearrange("p j (c i) -> p c j i", i=4))
+            cols = slice(u * HALF, (u + 1) * HALF)
+            nc.vector.quantize_mx(out=h_codes[:, cols].bitcast(FP8X4), scales=h_scales[:, cols], in_=grouped[:].rearrange("p w j -> p (w j)"))
+
+        for i in range(TILES):
+            nc.vector.tensor_reduce(stats[:, i, 1:2], a_sb[i][:], AX.X, ALU.max, negate=True)
+            nc.scalar.activation(ea[:, i, PAD:], a_sb[i][:], ACT.Exp, bias=stats[:, i, 1:2])
+
+        for i in range(TILES):
+            cols = slice(i * P, (i + 1) * P)
+            y_ps = psum.tile([P, S], F32, name="y_ps%d" % i, tag="row%d" % i)
+            nc.tensor.matmul_mx(out=y_ps[:], lhsT=h_codes[:, cols].bitcast(FP8X4), lhsT_scale=h_scales[:, cols],
+                                rhs=words[:].bitcast(FP8X4), rhs_scale=scales[:], start=True, stop=True)
+            nc.vector.tensor_scalar(y_sb[i][:, :S], y_ps[:], 1.0, None, ALU.mult, ALU.max, accum_out=stats[:, i, 0:1])
+            nc.scalar.mul(neg_ymax[:, i : i + 1], stats[:, i, 0:1], -1.0)
+            ee = keep.tile([P, BLOCKS * TILES, P], F32, name="ee%d" % i, tag="late")
+            nc.scalar.activation(ee[:, 0:BLOCKS, :].rearrange("p b t -> p (b t)"), y_sb[i][:, :S], ACT.Exp, bias=neg_ymax[:, i : i + 1], accum_out=sums[:, i : i + 1])
+
+        s_ps = []
+        for i in range(TILES):
+            p1 = keep.tile([P, R], F32, name="p1_%d" % i)
+            p2 = keep.tile([P, R], F32, name="p2_%d" % i)
+            (nc.gpsimd if (i, 1) in POOL_MASKS else nc.vector).tensor_tensor(p1[:], ea[:, i, PAD - 1 : PAD - 1 + R], m1_sb[:], ALU.mult)
+            (nc.gpsimd if (i, 2) in POOL_MASKS else nc.vector).tensor_tensor(p2[:], ea[:, i, PAD - 2 : PAD - 2 + R], m2_sb[:], ALU.mult)
+            bank = psum.tile([P, BLOCKS, P], F32, name="s_ps%d" % i)
+            terms = (ea[:, i, PAD:], p1[:], p2[:])
+            for n, term in enumerate(terms):
+                for b in range(BLOCKS):
+                    first, last = (n, b) == (0, 0), (n, b) == (len(terms) - 1, BLOCKS - 1)
+                    nc.tensor.matmul(bank[:, b, :], term[:, b * P : (b + 1) * P], ident[:], start=first, stop=last, is_transpose=True)
+            s_ps.append(bank)
+
+        picked = {}
+        for i in range(TILES):
+            if i not in FUSED:
+                picked[i] = keep.tile([P, R], F32, name="picked%d" % i)
+                for u in range(2):
+                    nc.vector.tensor_copy(picked[i][:, u * PIECE : (u + 1) * PIECE], y_sb[i][:].indirect(lab_sb[:, u * PIECE // 16 : (u + 1) * PIECE // 16]))
+
+        nc.scalar.activation(stats[:, :, 2], sums[:], ACT.Ln, scale=LN_SCALE)
+        nc.vector.tensor_reduce(shift[:], stats[:, :, 0:3], AX.X, ALU.add, negate=True)
+
+        log_t = keep.tile([P, BLOCKS * TILES, P], F32, name="log_t", tag="late")
+        for i in range(TILES):
+            nc.scalar.activation(log_t[:, i * BLOCKS : (i + 1) * BLOCKS, :], s_ps[i][:], ACT.Ln, scale=LN_SCALE)
+            l_ps = psum.tile([P, R], F32, name="l_ps%d" % i, tag="row%d" % i)
+            for b in range(BLOCKS):
+                nc.tensor.transpose(l_ps[:, b * P : (b + 1) * P], log_t[:, i * BLOCKS + b, :], ident[:])
+            res = keep.tile([P, R], F32, name="res%d" % i)
+            rows = slice(i * P, (i + 1) * P)
+            if i in FUSED:
+                l_sb = keep.tile([P, R], F32, name="l_sb%d" % i)
+                nc.scalar.activation(l_sb[:], l_ps[:], ACT.Identity, bias=shift[:, i : i + 1])
+                for u in range(2):
+                    cols = slice(u * PIECE, (u + 1) * PIECE)
+                    nc.vector.tensor_tensor(res[:, cols], y_sb[i][:].indirect(lab_sb[:, u * PIECE // 16 : (u + 1) * PIECE // 16]), l_sb[:, cols], ALU.add)
+            else:
+                nc.vector.scalar_tensor_tensor(res[:], l_ps[:], shift[:, i : i + 1], picked[i][:], ALU.add, ALU.add)
+            nc.sync.dma_start(out[rows, :], res[:])

@@ -12,136 +12,170 @@ U8 = mybir.dt.uint8
 FP8X4 = mybir.dt.float8_e4m3fn_x4
 ALU = mybir.AluOpType
 ACT = mybir.ActivationFunctionType
-AX = mybir.AxisListType
+AXIS = mybir.AxisListType
 
 P = 128
 PACK = 4
-K, T, S, V, R = 512, 1024, 512, 512, 512
-TILES = V // P
-BLOCKS = R // P
+QUADRANT = 32
+LIST_ROWS = 16
+K, SYMBOLS, PICKED, STREAMS, PLACES = 512, 1024, 512, 512, 512
+TILES = STREAMS // P
+BLOCKS = PLACES // P
 HALVES = 2
-HALF = V // HALVES
-PAD = 16
+HALF = STREAMS // HALVES
+REACH = 2
+LEAD = 16
+WINDOW = 704
 LN_SCALE = 2.0**54
+BANKS = 4
 
-POOL_MASKS = [(0, 1),(0, 2),(1, 1),(1, 2),(2, 1),(2, 2),(3, 1),(3, 2)]
-FUSED = []
-PIECE = R // 2
-
-FLOPS = 2 * K * V * S
+FLOPS = 2 * K * STREAMS * PICKED
 
 
 def tile_picked_yctc_log_p_kernel(tc, x_words, x_scales, hT, alpha, m1, m2, offs, lab, out):
     nc = tc.nc
     with ExitStack() as ctx:
         keep = ctx.enter_context(tc.tile_pool(name="keep", bufs=1))
-        psum = ctx.enter_context(tc.psum_pool(name="psum", bufs=1))
+        psum = ctx.enter_context(tc.psum_pool(name="psum", bufs=BANKS))
 
-        offs_sb = keep.tile([P, S // 16], U16, name="offs_sb")
-        lab_sb = keep.tile([P, R // 16], U16, name="lab_sb")
-        words_all = keep.tile([P, T], I32, name="words_all", align_bytes=64)
-        scales_all = keep.tile([P, T], U8, name="scales_all", align_bytes=64)
-        words = keep.tile([P, S], U32, name="words", align_bytes=64)
-        scales = keep.tile([P, S], U8, name="scales", align_bytes=64)
+        offs_sb = keep.tile([P, PICKED // LIST_ROWS], U16, name="offs_sb")
+        lab_sb = keep.tile([P, PLACES // LIST_ROWS], U16, name="lab_sb")
+        word_table = keep.tile([P, SYMBOLS], I32, name="word_table", tag="table", align_bytes=64)
+        scale_table = keep.tile([P, SYMBOLS], U8, name="scale_table", align_bytes=64)
+        x_codes = keep.tile([P, PICKED], U32, name="x_codes", align_bytes=64)
         ident = keep.tile([P, P], F32, name="ident")
-        warm = keep.tile([P, 2], F32, name="warm")
-
-        nc.gpsimd.memset(scales_all[:].bitcast(I32), 0)
-        nc.vector.memset(warm[:, 0:1], 0.0)
-        nc.scalar.activation(warm[:, 1:2], warm[:, 0:1], ACT.Exp)
-
-        h_view = hT.rearrange("(p j) t -> p j t", j=PACK)
+        zeros = keep.tile([P, TILES, REACH], F32, name="zeros")
         h_raw = [keep.tile([P, PACK, HALF], F32, name="h_raw%d" % u) for u in range(HALVES)]
-        a_sb = [keep.tile([P, R], F32, name="a_sb%d" % i) for i in range(TILES)]
-        m1_sb = keep.tile([P, R], F32, name="m1_sb")
-        m2_sb = keep.tile([P, R], F32, name="m2_sb")
+        alpha_sb = [keep.tile([P, PLACES], F32, name="alpha_sb%d" % i) for i in range(TILES)]
+        allowed = [keep.tile([P, PLACES], F32, name="allowed%d" % n) for n in range(REACH)]
+        ea = keep.tile([P, TILES, LEAD + PLACES], F32, name="ea")
+
+        nc.gpsimd.memset(scale_table[:].bitcast(I32), 0)
+        nc.gpsimd.memset(zeros[:], 0.0)
+        nc.scalar.activation(ea[:, :, LEAD - REACH : LEAD], zeros[:], ACT.Copy)
+
+        def load_alpha(i):
+            nc.sync.dma_start(alpha_sb[i][:], alpha[i * P : (i + 1) * P, :])
+
         nc.sync.dma_start(offs_sb[:], offs)
-        nc.sync.dma_start(a_sb[0][:], alpha[0 * P : 1 * P, :])
-        for q in range(4):
-            nc.scalar.dma_start(scales_all[32 * q : 32 * q + 4, :].bitcast(I32), x_scales[0, 4 * q : 4 * q + 4, :].bitcast(I32))
-        nc.sync.dma_start(m1_sb[:], m1)
-        nc.sync.dma_start(words_all[:], x_words[0].rearrange("p n t -> p (n t)").bitcast(I32))
-        nc.sync.dma_start(m2_sb[:], m2)
-        nc.sync.dma_start(h_raw[0][:], h_view[:, :, 0 * HALF : 1 * HALF])
-        nc.sync.dma_start(a_sb[1][:], alpha[1 * P : 2 * P, :])
-        nc.sync.dma_start(h_raw[1][:], h_view[:, :, 1 * HALF : 2 * HALF])
-        nc.sync.dma_start(a_sb[2][:], alpha[2 * P : 3 * P, :])
-        nc.sync.dma_start(a_sb[3][:], alpha[3 * P : 4 * P, :])
+        load_alpha(0)
+        nc.sync.dma_start(word_table[:], x_words[0].rearrange("p n j -> p (n j)").bitcast(I32))
+        nc.sync.dma_start(allowed[0][:], m1)
+        for q in range(P // QUADRANT):
+            nc.sync.dma_start(
+                scale_table[QUADRANT * q : QUADRANT * q + 4, :].bitcast(I32), x_scales[0, 4 * q : 4 * q + 4, :].bitcast(I32)
+            )
+        nc.sync.dma_start(allowed[1][:], m2)
+        h_rows = hT.rearrange("(p j) t -> p j t", j=PACK)
+        for u in range(HALVES):
+            nc.sync.dma_start(h_raw[u][:], h_rows[:, :, u * HALF : (u + 1) * HALF])
+            load_alpha(u + 1)
+        for i in range(HALVES + 1, TILES):
+            load_alpha(i)
         nc.sync.dma_start(lab_sb[:], lab)
 
         make_identity(nc, ident[:])
-        ea = keep.tile([P, TILES, PAD + R], F32, name="ea")
-        nc.gpsimd.memset(ea[:, :, PAD - 2 : PAD], 0.0)
-        y_sb = [keep.tile([P, S], F32, name="y_sb%d" % i) for i in range(TILES)]
+        neg_y = [keep.tile([P, WINDOW], F32, name="neg_y%d" % i) for i in range(TILES)]
+        for i in range(TILES):
+            nc.gpsimd.memset(neg_y[i][:, PICKED:], 0.0)
 
-        nc.vector.tensor_copy(scales[:], scales_all[:].indirect(offs_sb[:]))
-        nc.vector.tensor_copy(words[:], words_all[:].bitcast(U32).indirect(offs_sb[:]))
-
-        stats = keep.tile([P, TILES, 4], F32, name="stats")
-        neg_ymax = keep.tile([P, TILES], F32, name="neg_ymax")
+        neg_alpha_max = keep.tile([P, TILES], F32, name="neg_alpha_max")
+        neg_y_max = keep.tile([P, TILES], F32, name="neg_y_max")
+        max_gap = keep.tile([P, TILES], F32, name="max_gap")
         sums = keep.tile([P, TILES], F32, name="sums")
+        log_sums = keep.tile([P, TILES], F32, name="log_sums")
         shift = keep.tile([P, TILES], F32, name="shift")
+        h_codes = keep.tile([P, STREAMS], U32, name="h_codes", align_bytes=64)
+        h_scales = keep.tile([P, STREAMS], U8, name="h_scales", align_bytes=64)
 
-        h_codes = keep.tile([P, V], U32, name="h_codes", align_bytes=64)
-        h_scales = keep.tile([P, V], U8, name="h_scales", align_bytes=64)
-        for u in range(HALVES):
+        def exp_alpha(i):
+            nc.vector.tensor_reduce(neg_alpha_max[:, i : i + 1], alpha_sb[i][:], AXIS.X, ALU.max, negate=True)
+            nc.scalar.activation(ea[:, i, LEAD:], alpha_sb[i][:], ACT.Exp, bias=neg_alpha_max[:, i : i + 1])
+
+        def quantize(u):
             grouped = keep.tile([P, HALF, PACK], BF16, name="grouped%d" % u, align_bytes=64)
-            nc.scalar.copy(grouped[:].rearrange("p (c i) j -> p c j i", i=4), h_raw[u][:].rearrange("p j (c i) -> p c j i", i=4))
+            nc.scalar.copy(grouped[:].rearrange("p (c e) j -> p c j e", e=4), h_raw[u][:].rearrange("p j (c e) -> p c j e", e=4))
             cols = slice(u * HALF, (u + 1) * HALF)
-            nc.vector.quantize_mx(out=h_codes[:, cols].bitcast(FP8X4), scales=h_scales[:, cols], in_=grouped[:].rearrange("p w j -> p (w j)"))
+            nc.vector.quantize_mx(
+                out=h_codes[:, cols].bitcast(FP8X4), scales=h_scales[:, cols], in_=grouped[:].rearrange("p t j -> p (t j)")
+            )
 
-        for i in range(TILES):
-            nc.vector.tensor_reduce(stats[:, i, 1:2], a_sb[i][:], AX.X, ALU.max, negate=True)
-            nc.scalar.activation(ea[:, i, PAD:], a_sb[i][:], ACT.Exp, bias=stats[:, i, 1:2])
-
-        for i in range(TILES):
+        def logits(i):
             cols = slice(i * P, (i + 1) * P)
-            y_ps = psum.tile([P, S], F32, name="y_ps%d" % i, tag="row%d" % i)
-            nc.tensor.matmul_mx(out=y_ps[:], lhsT=h_codes[:, cols].bitcast(FP8X4), lhsT_scale=h_scales[:, cols],
-                                rhs=words[:].bitcast(FP8X4), rhs_scale=scales[:], start=True, stop=True)
-            nc.vector.tensor_scalar(y_sb[i][:, :S], y_ps[:], 1.0, None, ALU.mult, ALU.max, accum_out=stats[:, i, 0:1])
-            nc.scalar.mul(neg_ymax[:, i : i + 1], stats[:, i, 0:1], -1.0)
-            ee = keep.tile([P, BLOCKS * TILES, P], F32, name="ee%d" % i, tag="late")
-            nc.scalar.activation(ee[:, 0:BLOCKS, :].rearrange("p b t -> p (b t)"), y_sb[i][:, :S], ACT.Exp, bias=neg_ymax[:, i : i + 1], accum_out=sums[:, i : i + 1])
+            y = psum.tile([P, PICKED], F32, name="y%d" % i, tag="rows")
+            nc.tensor.matmul_mx(
+                out=y[:],
+                lhsT=h_codes[:, cols].bitcast(FP8X4),
+                lhsT_scale=h_scales[:, cols],
+                rhs=x_codes[:].bitcast(FP8X4),
+                rhs_scale=x_scale_bytes[:],
+                start=True,
+                stop=True,
+            )
+            nc.vector.tensor_scalar(neg_y[i][:, :PICKED], y[:], -1.0, None, ALU.mult, ALU.min, accum_out=neg_y_max[:, i : i + 1])
+            ee = keep.tile([P, PICKED], F32, name="ee%d" % i, tag="exp_then_log")
+            nc.scalar.activation(
+                ee[:], neg_y[i][:, :PICKED], ACT.Exp, bias=neg_y_max[:, i : i + 1], scale=-1.0, accum_out=sums[:, i : i + 1]
+            )
 
-        s_ps = []
-        for i in range(TILES):
-            p1 = keep.tile([P, R], F32, name="p1_%d" % i)
-            p2 = keep.tile([P, R], F32, name="p2_%d" % i)
-            (nc.gpsimd if (i, 1) in POOL_MASKS else nc.vector).tensor_tensor(p1[:], ea[:, i, PAD - 1 : PAD - 1 + R], m1_sb[:], ALU.mult)
-            (nc.gpsimd if (i, 2) in POOL_MASKS else nc.vector).tensor_tensor(p2[:], ea[:, i, PAD - 2 : PAD - 2 + R], m2_sb[:], ALU.mult)
-            bank = psum.tile([P, BLOCKS, P], F32, name="s_ps%d" % i)
-            terms = (ea[:, i, PAD:], p1[:], p2[:])
+        def three_terms(i):
+            terms = [ea[:, i, LEAD:]]
+            for n in range(REACH):
+                product = keep.tile([P, PLACES], F32, name="product%d_%d" % (n, i))
+                first = LEAD - 1 - n
+                nc.gpsimd.tensor_tensor(product[:], ea[:, i, first : first + PLACES], allowed[n][:], ALU.mult)
+                terms.append(product[:])
+            return terms
+
+        def sum_transposed(i, terms):
+            bank = psum.tile([P, BLOCKS, P], F32, name="sum_t%d" % i, tag="sums")
             for n, term in enumerate(terms):
                 for b in range(BLOCKS):
-                    first, last = (n, b) == (0, 0), (n, b) == (len(terms) - 1, BLOCKS - 1)
-                    nc.tensor.matmul(bank[:, b, :], term[:, b * P : (b + 1) * P], ident[:], start=first, stop=last, is_transpose=True)
-            s_ps.append(bank)
+                    nc.tensor.matmul(
+                        bank[:, b, :],
+                        term[:, b * P : (b + 1) * P],
+                        ident[:],
+                        start=(n == 0 and b == 0),
+                        stop=(n == len(terms) - 1 and b == BLOCKS - 1),
+                        is_transpose=True,
+                    )
+            return bank
 
-        picked = {}
+        def look_up(i):
+            picked = keep.tile([P, PLACES], F32, name="picked%d" % i)
+            nc.vector.tensor_copy(picked[:], neg_y[i][:].indirect(lab_sb[:]))
+            return picked
+
+        exp_alpha(0)
+        nc.vector.tensor_copy(x_codes[:], word_table[:].bitcast(U32).indirect(offs_sb[:]))
+        x_scale_bytes = keep.tile([P, PICKED], U8, name="x_scale_bytes", tag="table", align_bytes=64)
+        nc.vector.tensor_copy(x_scale_bytes[:], scale_table[:].indirect(offs_sb[:]))
+        for u in range(HALVES):
+            quantize(u)
+            exp_alpha(u + 1)
+        for i in range(HALVES + 1, TILES):
+            exp_alpha(i)
         for i in range(TILES):
-            if i not in FUSED:
-                picked[i] = keep.tile([P, R], F32, name="picked%d" % i)
-                for u in range(2):
-                    nc.vector.tensor_copy(picked[i][:, u * PIECE : (u + 1) * PIECE], y_sb[i][:].indirect(lab_sb[:, u * PIECE // 16 : (u + 1) * PIECE // 16]))
+            logits(i)
+        terms = [three_terms(i) for i in range(TILES)]
+        sum_t = [sum_transposed(i, terms[i]) for i in range(TILES)]
 
-        nc.scalar.activation(stats[:, :, 2], sums[:], ACT.Ln, scale=LN_SCALE)
-        nc.vector.tensor_reduce(shift[:], stats[:, :, 0:3], AX.X, ALU.add, negate=True)
+        nc.vector.tensor_tensor(max_gap[:], neg_y_max[:], neg_alpha_max[:], ALU.subtract)
+        neg_picked = [look_up(i) for i in range(TILES)]
+        nc.scalar.activation(log_sums[:], sums[:], ACT.Ln, scale=LN_SCALE)
+        nc.vector.tensor_tensor(shift[:], max_gap[:], log_sums[:], ALU.subtract)
 
-        log_t = keep.tile([P, BLOCKS * TILES, P], F32, name="log_t", tag="late")
+        log_t = keep.tile([P, TILES, BLOCKS, P], F32, name="log_t", tag="exp_then_log")
         for i in range(TILES):
-            nc.scalar.activation(log_t[:, i * BLOCKS : (i + 1) * BLOCKS, :], s_ps[i][:], ACT.Ln, scale=LN_SCALE)
-            l_ps = psum.tile([P, R], F32, name="l_ps%d" % i, tag="row%d" % i)
-            for b in range(BLOCKS):
-                nc.tensor.transpose(l_ps[:, b * P : (b + 1) * P], log_t[:, i * BLOCKS + b, :], ident[:])
-            res = keep.tile([P, R], F32, name="res%d" % i)
-            rows = slice(i * P, (i + 1) * P)
-            if i in FUSED:
-                l_sb = keep.tile([P, R], F32, name="l_sb%d" % i)
-                nc.scalar.activation(l_sb[:], l_ps[:], ACT.Identity, bias=shift[:, i : i + 1])
-                for u in range(2):
-                    cols = slice(u * PIECE, (u + 1) * PIECE)
-                    nc.vector.tensor_tensor(res[:, cols], y_sb[i][:].indirect(lab_sb[:, u * PIECE // 16 : (u + 1) * PIECE // 16]), l_sb[:, cols], ALU.add)
-            else:
-                nc.vector.scalar_tensor_tensor(res[:], l_ps[:], shift[:, i : i + 1], picked[i][:], ALU.add, ALU.add)
-            nc.sync.dma_start(out[rows, :], res[:])
+            result = keep.tile([P, PLACES], F32, name="result%d" % i)
+            step = BLOCKS // 2 if i == TILES - 1 else BLOCKS
+            for b0 in range(0, BLOCKS, step):
+                cols = slice(b0 * P, (b0 + step) * P)
+                nc.scalar.activation(log_t[:, i, b0 : b0 + step, :], sum_t[i][:, b0 : b0 + step, :], ACT.Ln, scale=LN_SCALE)
+                log_rows = psum.tile([P, step * P], F32, name="log_rows%d_%d" % (i, b0), tag="sums" if b0 else "rows")
+                for b in range(step):
+                    nc.tensor.transpose(log_rows[:, b * P : (b + 1) * P], log_t[:, i, b0 + b, :], ident[:])
+                nc.vector.scalar_tensor_tensor(
+                    result[:, cols], log_rows[:], shift[:, i : i + 1], neg_picked[i][:, cols], ALU.add, ALU.subtract
+                )
+                nc.sync.dma_start(out[i * P : (i + 1) * P, cols], result[:, cols])

from contextlib import ExitStack

import concourse.mybir as mybir
from concourse.masks import make_identity

F32 = mybir.dt.float32
BF16 = mybir.dt.bfloat16
I32 = mybir.dt.int32
U32 = mybir.dt.uint32
U16 = mybir.dt.uint16
U8 = mybir.dt.uint8
FP8X4 = mybir.dt.float8_e4m3fn_x4
ALU = mybir.AluOpType
ACT = mybir.ActivationFunctionType
AXIS = mybir.AxisListType

P = 128
PACK = 4
QUADRANT = 32
LIST_ROWS = 16
K, SYMBOLS, PICKED, STREAMS, PLACES = 512, 1024, 512, 512, 512
TILES = STREAMS // P
BLOCKS = PLACES // P
HALVES = 2
HALF = STREAMS // HALVES
REACH = 2
LEAD = 16
WINDOW = 704
LN_SCALE = 2.0**54
BANKS = 4

FLOPS = 2 * K * STREAMS * PICKED


def tile_picked_yctc_log_p_kernel(tc, x_words, x_scales, hT, alpha, m1, m2, offs, lab, out):
    nc = tc.nc
    with ExitStack() as ctx:
        keep = ctx.enter_context(tc.tile_pool(name="keep", bufs=1))
        psum = ctx.enter_context(tc.psum_pool(name="psum", bufs=BANKS))

        offs_sb = keep.tile([P, PICKED // LIST_ROWS], U16, name="offs_sb")
        lab_sb = keep.tile([P, PLACES // LIST_ROWS], U16, name="lab_sb")
        word_table = keep.tile([P, SYMBOLS], I32, name="word_table", tag="table", align_bytes=64)
        scale_table = keep.tile([P, SYMBOLS], U8, name="scale_table", align_bytes=64)
        x_codes = keep.tile([P, PICKED], U32, name="x_codes", align_bytes=64)
        ident = keep.tile([P, P], F32, name="ident")
        zeros = keep.tile([P, TILES, REACH], F32, name="zeros")
        h_raw = [keep.tile([P, PACK, HALF], F32, name="h_raw%d" % u) for u in range(HALVES)]
        alpha_sb = [keep.tile([P, PLACES], F32, name="alpha_sb%d" % i) for i in range(TILES)]
        allowed = [keep.tile([P, PLACES], F32, name="allowed%d" % n) for n in range(REACH)]
        ea = keep.tile([P, TILES, LEAD + PLACES], F32, name="ea")

        nc.gpsimd.memset(scale_table[:].bitcast(I32), 0)
        nc.gpsimd.memset(zeros[:], 0.0)
        nc.scalar.activation(ea[:, :, LEAD - REACH : LEAD], zeros[:], ACT.Copy)

        def load_alpha(i):
            nc.sync.dma_start(alpha_sb[i][:], alpha[i * P : (i + 1) * P, :])

        nc.sync.dma_start(offs_sb[:], offs)
        load_alpha(0)
        nc.sync.dma_start(word_table[:], x_words[0].rearrange("p n j -> p (n j)").bitcast(I32))
        nc.sync.dma_start(allowed[0][:], m1)
        for q in range(P // QUADRANT):
            nc.sync.dma_start(
                scale_table[QUADRANT * q : QUADRANT * q + 4, :].bitcast(I32), x_scales[0, 4 * q : 4 * q + 4, :].bitcast(I32)
            )
        nc.sync.dma_start(allowed[1][:], m2)
        h_rows = hT.rearrange("(p j) t -> p j t", j=PACK)
        for u in range(HALVES):
            nc.sync.dma_start(h_raw[u][:], h_rows[:, :, u * HALF : (u + 1) * HALF])
            load_alpha(u + 1)
        for i in range(HALVES + 1, TILES):
            load_alpha(i)
        nc.sync.dma_start(lab_sb[:], lab)

        make_identity(nc, ident[:])
        neg_y = [keep.tile([P, WINDOW], F32, name="neg_y%d" % i) for i in range(TILES)]
        for i in range(TILES):
            nc.gpsimd.memset(neg_y[i][:, PICKED:], 0.0)

        neg_alpha_max = keep.tile([P, TILES], F32, name="neg_alpha_max")
        neg_y_max = keep.tile([P, TILES], F32, name="neg_y_max")
        max_gap = keep.tile([P, TILES], F32, name="max_gap")
        sums = keep.tile([P, TILES], F32, name="sums")
        log_sums = keep.tile([P, TILES], F32, name="log_sums")
        shift = keep.tile([P, TILES], F32, name="shift")
        h_codes = keep.tile([P, STREAMS], U32, name="h_codes", align_bytes=64)
        h_scales = keep.tile([P, STREAMS], U8, name="h_scales", align_bytes=64)

        def exp_alpha(i):
            nc.vector.tensor_reduce(neg_alpha_max[:, i : i + 1], alpha_sb[i][:], AXIS.X, ALU.max, negate=True)
            nc.scalar.activation(ea[:, i, LEAD:], alpha_sb[i][:], ACT.Exp, bias=neg_alpha_max[:, i : i + 1])

        def quantize(u):
            grouped = keep.tile([P, HALF, PACK], BF16, name="grouped%d" % u, align_bytes=64)
            nc.scalar.copy(grouped[:].rearrange("p (c e) j -> p c j e", e=4), h_raw[u][:].rearrange("p j (c e) -> p c j e", e=4))
            cols = slice(u * HALF, (u + 1) * HALF)
            nc.vector.quantize_mx(
                out=h_codes[:, cols].bitcast(FP8X4), scales=h_scales[:, cols], in_=grouped[:].rearrange("p t j -> p (t j)")
            )

        def logits(i):
            cols = slice(i * P, (i + 1) * P)
            y = psum.tile([P, PICKED], F32, name="y%d" % i, tag="rows")
            nc.tensor.matmul_mx(
                out=y[:],
                lhsT=h_codes[:, cols].bitcast(FP8X4),
                lhsT_scale=h_scales[:, cols],
                rhs=x_codes[:].bitcast(FP8X4),
                rhs_scale=x_scale_bytes[:],
                start=True,
                stop=True,
            )
            nc.vector.tensor_scalar(neg_y[i][:, :PICKED], y[:], -1.0, None, ALU.mult, ALU.min, accum_out=neg_y_max[:, i : i + 1])
            ee = keep.tile([P, PICKED], F32, name="ee%d" % i, tag="exp_then_log")
            nc.scalar.activation(
                ee[:], neg_y[i][:, :PICKED], ACT.Exp, bias=neg_y_max[:, i : i + 1], scale=-1.0, accum_out=sums[:, i : i + 1]
            )

        def three_terms(i):
            terms = [ea[:, i, LEAD:]]
            for n in range(REACH):
                product = keep.tile([P, PLACES], F32, name="product%d_%d" % (n, i))
                first = LEAD - 1 - n
                nc.gpsimd.tensor_tensor(product[:], ea[:, i, first : first + PLACES], allowed[n][:], ALU.mult)
                terms.append(product[:])
            return terms

        def sum_transposed(i, terms):
            bank = psum.tile([P, BLOCKS, P], F32, name="sum_t%d" % i, tag="sums")
            for n, term in enumerate(terms):
                for b in range(BLOCKS):
                    nc.tensor.matmul(
                        bank[:, b, :],
                        term[:, b * P : (b + 1) * P],
                        ident[:],
                        start=(n == 0 and b == 0),
                        stop=(n == len(terms) - 1 and b == BLOCKS - 1),
                        is_transpose=True,
                    )
            return bank

        def look_up(i):
            picked = keep.tile([P, PLACES], F32, name="picked%d" % i)
            nc.vector.tensor_copy(picked[:], neg_y[i][:].indirect(lab_sb[:]))
            return picked

        exp_alpha(0)
        nc.vector.tensor_copy(x_codes[:], word_table[:].bitcast(U32).indirect(offs_sb[:]))
        x_scale_bytes = keep.tile([P, PICKED], U8, name="x_scale_bytes", tag="table", align_bytes=64)
        nc.vector.tensor_copy(x_scale_bytes[:], scale_table[:].indirect(offs_sb[:]))
        for u in range(HALVES):
            quantize(u)
            exp_alpha(u + 1)
        for i in range(HALVES + 1, TILES):
            exp_alpha(i)
        for i in range(TILES):
            logits(i)
        terms = [three_terms(i) for i in range(TILES)]
        sum_t = [sum_transposed(i, terms[i]) for i in range(TILES)]

        nc.vector.tensor_tensor(max_gap[:], neg_y_max[:], neg_alpha_max[:], ALU.subtract)
        neg_picked = [look_up(i) for i in range(TILES)]
        nc.scalar.activation(log_sums[:], sums[:], ACT.Ln, scale=LN_SCALE)
        nc.vector.tensor_tensor(shift[:], max_gap[:], log_sums[:], ALU.subtract)

        log_t = keep.tile([P, TILES, BLOCKS, P], F32, name="log_t", tag="exp_then_log")
        for i in range(TILES):
            result = keep.tile([P, PLACES], F32, name="result%d" % i)
            step = BLOCKS // 2 if i == TILES - 1 else BLOCKS
            for b0 in range(0, BLOCKS, step):
                cols = slice(b0 * P, (b0 + step) * P)
                nc.scalar.activation(log_t[:, i, b0 : b0 + step, :], sum_t[i][:, b0 : b0 + step, :], ACT.Ln, scale=LN_SCALE)
                log_rows = psum.tile([P, step * P], F32, name="log_rows%d_%d" % (i, b0), tag="sums" if b0 else "rows")
                for b in range(step):
                    nc.tensor.transpose(log_rows[:, b * P : (b + 1) * P], log_t[:, i, b0 + b, :], ident[:])
                nc.vector.scalar_tensor_tensor(
                    result[:, cols], log_rows[:], shift[:, i : i + 1], neg_picked[i][:, cols], ALU.add, ALU.subtract
                )
                nc.sync.dma_start(out[i * P : (i + 1) * P, cols], result[:, cols])
